import numpy as np
import ml_dtypes


def mxq(x, axis, fmt="e4m3"):
    dtype, down = {"e4m3": (ml_dtypes.float8_e4m3fn, 7), "e5m2": (ml_dtypes.float8_e5m2, 14)}[fmt]
    v = np.moveaxis(np.asarray(x, np.float32).astype(ml_dtypes.bfloat16).astype(np.float64), axis, -1)
    blocks = v.reshape(v.shape[:-1] + (-1, 32))
    amax = np.abs(blocks).max(-1, keepdims=True)
    byte = np.maximum(np.where(amax > 0, np.frexp(amax)[1] - 1 + 127, 0) - down, 1)
    scale = np.exp2(byte - 127.0)
    codes = (blocks / scale).astype(np.float32).astype(dtype).astype(np.float64)
    return np.moveaxis((codes * scale).reshape(v.shape), -1, axis)


WIDE = False


def mx_kscale(k):
    if not WIDE:
        return np.ones(k)
    levels = np.array([10, -10, 5, -5, 0])
    if k % 512:
        return np.exp2(np.random.permutation(np.resize(levels, k // 32))).repeat(32)
    a = np.empty((k // 512, 16))
    for p in range(k // 512):
        a[p, :8] = np.random.permutation(np.resize(levels, 8))
        for g in range(8):
            far = levels[np.abs(levels - a[p, g]) >= 10]
            a[p, g + 8] = far[np.random.randint(len(far))]
    return np.exp2(a.ravel()).repeat(32)


def f64(x):
    return np.asarray(x).astype(np.float64)


def striped(idx):
    return np.tile(idx.reshape(-1, 16).T, (8, 1)).astype(np.uint16)


def unstriped(offs):
    return offs[:16].T.reshape(-1).astype(np.int64)


def striped8(idx):
    return np.concatenate([x.reshape(-1, 16).T for x in idx]).astype(np.uint16)


def runs(offs, k):
    lists = np.stack([offs[16 * r : 16 * r + 16].T.reshape(-1) for r in range(8)]).astype(np.int64)
    return lists[np.arange(k) % 512 // 64]


def pack_weight(w):
    k, n = w.shape
    w = f64(np.asarray(w, np.float32).astype(ml_dtypes.bfloat16)).reshape(k // 32, 32, n)
    amax = np.abs(w).max(1)
    byte = np.clip(np.where(amax > 0, np.frexp(amax)[1] - 1 + 127 - 7, 1), 1, 254)
    scaled = (w * np.exp2(127.0 - byte)[:, None, :]).reshape(k, n).astype(np.float32)
    words = np.ascontiguousarray(scaled.reshape(k // 512, 128, 4, n).transpose(0, 1, 3, 2)).astype(ml_dtypes.float8_e4m3fn).view(np.uint8)
    return words, np.ascontiguousarray(byte.astype(np.uint8).reshape(k // 512, 16, n))


def unpack_weight(words, scales):
    g, p, n, _ = words.shape
    vals = np.ascontiguousarray(words).view(ml_dtypes.float8_e4m3fn).astype(np.float64) * np.repeat(np.exp2(scales.astype(np.float64) - 127.0), 8, axis=1)[..., None]
    return vals.transpose(0, 1, 3, 2).reshape(g * 512, n)


K, T, S, N, G, H = 512, 2048, 512, 512, 2048, 512


def setup_inputs():
    n = np.random.standard_normal
    s = mx_kscale(K)[:, None]
    u = mx_kscale(H)
    packed_xT = pack_weight(n((K, T)) * s)
    packed_dT = pack_weight(n((K, G)) / s)
    return {
        "x_words": packed_xT[0],
        "x_scales": packed_xT[1],
        "d_words": packed_dT[0],
        "d_scales": packed_dT[1],
        "gn": (np.random.uniform(0.5, 1.5, (H, 1)) * u[:, None]).astype(np.float32),
        "w1": (n((H, N)) / np.sqrt(H) / u[:, None]).astype(np.float32),
        "offs": striped(np.random.permutation(T)[:S]),
        "kidx": striped8(np.random.randint(0, G, (8, H))),
        "n1": striped8(np.stack([np.random.permutation(S) for _ in range(8)])),
        "n2": striped8(np.stack([np.random.permutation(S) for _ in range(8)])),
    }


def reference(x_words, x_scales, d_words, d_scales, gn, w1, offs, kidx, n1, n2):
    d_kidx = unpack_weight(d_words, d_scales)[np.arange(K)[:, None], runs(kidx, K)]
    xq = unpack_weight(x_words, x_scales)[:, unstriped(offs)]
    s = 0.0625 * (d_kidx.T @ xq)
    ex = np.exp(0.5 * s)
    z = f64(gn) * ((2.0 * ex) / (ex + ex[np.arange(H)[:, None], runs(n1, H)] + ex[np.arange(H)[:, None], runs(n2, H)]))
    return mxq(f64(w1), 0, "e4m3").T @ mxq(z, 0, "e4m3")

@@ -1,0 +1,175 @@
+from contextlib import ExitStack
+
+import concourse.mybir as mybir
+
+K, T, S, N, G, H = 512, 2048, 512, 512, 2048, 512
+FLOPS = 2 * K * H * S + 2 * H * N * S
+
+F32 = mybir.dt.float32
+BF16 = mybir.dt.bfloat16
+I32 = mybir.dt.int32
+U32 = mybir.dt.uint32
+U16 = mybir.dt.uint16
+U8 = mybir.dt.uint8
+FP8X4 = mybir.dt.float8_e4m3fn_x4
+ACT = mybir.ActivationFunctionType
+ALU = mybir.AluOpType
+
+P = 128
+PACK = 4
+LIST_ROWS = 16
+HALF = S // 2
+CHUNKS = ((0, 256), (256, 128), (384, 128))
+W_PIECES = 2
+
+
+def tile_picked_localsm_none_p_kernel(tc, x_words, x_scales, d_words, d_scales, gn, w1, offs, kidx, n1, n2, out):
+    nc = tc.nc
+    with ExitStack() as ctx:
+        lists = ctx.enter_context(tc.tile_pool(name="lists", bufs=1))
+        keep = ctx.enter_context(tc.tile_pool(name="keep", bufs=1))
+        psum = ctx.enter_context(tc.psum_pool(name="psum", bufs=1))
+
+        kidx_sb = lists.tile([P, H // LIST_ROWS], U16, name="kidx_sb")
+        offs_sb = lists.tile([P, S // LIST_ROWS], U16, name="offs_sb")
+        n1_sb = lists.tile([P, S // LIST_ROWS], U16, name="n1_sb")
+        n2_sb = lists.tile([P, S // LIST_ROWS], U16, name="n2_sb")
+        d_byte_table = keep.tile([P, G], U8, name="d_byte_table")
+        x_byte_table = keep.tile([P, T], U8, name="x_byte_table", tag="x_bytes_then_gn")
+        d_word_table = keep.tile([P, G], U32, name="d_word_table")
+        x_word_table = keep.tile([P, T], U32, name="x_word_table", tag="x_words_then_w", align_bytes=64)
+
+        nc.sync.dma_start(kidx_sb[:], kidx)
+        nc.sync.dma_start(
+            d_byte_table[:].bitcast(I32),
+            d_scales[0].bitcast(I32).unsqueeze(1).to_broadcast([16, 8, G // 4]),
+        )
+        nc.sync.dma_start(offs_sb[:], offs)
+        nc.sync.dma_start(
+            x_byte_table[:].bitcast(I32),
+            x_scales[0].bitcast(I32).unsqueeze(1).to_broadcast([16, 8, T // 4]),
+        )
+        nc.sync.dma_start(n1_sb[:], n1)
+        nc.sync.dma_start(n2_sb[:], n2)
+        nc.sync.dma_start(d_word_table[:].bitcast(I32), d_words[0].rearrange("p n r -> p (n r)").bitcast(I32))
+        nc.sync.dma_start(x_word_table[:].bitcast(I32), x_words[0].rearrange("p n r -> p (n r)").bitcast(I32))
+        w_width = N // W_PIECES
+        w_raw = []
+        for piece in range(W_PIECES):
+            raw = keep.tile([P, PACK, w_width], F32, name=f"w_raw{piece}")
+            nc.sync.dma_start(raw[:], w1[:, piece * w_width : (piece + 1) * w_width].rearrange("(p j) n -> p j n", j=PACK))
+            w_raw.append(raw)
+
+        d_bytes_picked = keep.tile([P, H], U8, name="d_bytes_picked")
+        nc.vector.tensor_copy(d_bytes_picked[:], d_byte_table[:].indirect(kidx_sb[:]))
+        x_bytes_picked = keep.tile([P, S], U8, name="x_bytes_picked")
+        nc.vector.tensor_copy(x_bytes_picked[:], x_byte_table[:].indirect(offs_sb[:]))
+        planes = keep.tile([P, H + S], U8, name="planes", align_bytes=64)
+        nc.vector.tensor_copy(
+            planes[:, :H].rearrange("p (t m) -> p m t", t=PACK),
+            d_bytes_picked[:].rearrange("p (m t) -> p m t", t=PACK),
+        )
+        nc.vector.tensor_copy(planes[:, H:].bitcast(I32), x_bytes_picked[:].bitcast(I32))
+        for r in range(1, 4):
+            nc.scalar.dma_start(planes[r:P:32, :].bitcast(I32), planes[8 * r : P : 32, :].bitcast(I32))
+        gn_sb = keep.tile([P, PACK], F32, name="gn_sb", tag="x_bytes_then_gn")
+        nc.sync.dma_start(gn_sb[:], gn.rearrange("(p t) o -> p (t o)", t=PACK))
+
+        d_codes_picked = keep.tile([P, H], U32, name="d_codes_picked")
+        nc.vector.tensor_copy(d_codes_picked[:], d_word_table[:].indirect(kidx_sb[:]))
+        d_codes = keep.tile([P, H], U32, name="d_codes", align_bytes=64)
+        nc.vector.tensor_copy(
+            d_codes[:].rearrange("p (t m) -> p t m", t=PACK),
+            d_codes_picked[:].rearrange("p (m t) -> p t m", t=PACK),
+        )
+        x_codes = keep.tile([P, S], U32, name="x_codes", align_bytes=64)
+        nc.vector.tensor_copy(x_codes[:], x_word_table[:].indirect(offs_sb[:]))
+
+        w_codes = keep.tile([P, N], U32, name="w_codes", align_bytes=64)
+        w_bytes = keep.tile([P, N], U8, name="w_bytes", align_bytes=64)
+        w_grouped = keep.tile([P, N, PACK], BF16, name="w_grouped", tag="x_words_then_w", align_bytes=64)
+        for piece in range(W_PIECES):
+            cols = slice(piece * w_width, (piece + 1) * w_width)
+            nc.vector.tensor_copy(w_grouped[:, cols, :], w_raw[piece][:].rearrange("p j n -> p n j"))
+        for piece in range(W_PIECES):
+            cols = slice(piece * w_width, (piece + 1) * w_width)
+            nc.vector.quantize_mx(
+                out=w_codes[:, cols].bitcast(FP8X4),
+                scales=w_bytes[:, cols],
+                in_=w_grouped[:, cols, :].rearrange("p n j -> p (n j)"),
+            )
+
+        ex_table = []
+        ex_plain = []
+        for t in range(PACK):
+            keys = slice(t * P, (t + 1) * P)
+            scores = psum.tile([P, S], F32, name=f"scores{t}")
+            nc.tensor.matmul_mx(
+                out=scores[:],
+                lhsT=d_codes[:, keys].bitcast(FP8X4),
+                lhsT_scale=planes[:, keys],
+                rhs=x_codes[:].bitcast(FP8X4),
+                rhs_scale=planes[:, H:],
+                start=True,
+                stop=True,
+            )
+            table = keep.tile([P, S], F32, name=f"ex_table{t}")
+            plain = keep.tile([P, S], F32, name=f"ex_plain{t}")
+            nc.scalar.activation(table[:], scores[:], ACT.Exp, scale=0.03125)
+            nc.scalar.activation(plain[:], scores[:], ACT.Exp, scale=0.03125)
+            ex_table.append(table)
+            ex_plain.append(plain)
+
+        den = []
+        for t in range(PACK):
+            pair = keep.tile([P, S], F32, name=f"pair{t}")
+            total = keep.tile([P, S], F32, name=f"den{t}")
+            for other, target, lst in ((ex_plain[t], pair, n1_sb), (pair, total, n2_sb)):
+                for h in range(2):
+                    cols = slice(h * HALF, (h + 1) * HALF)
+                    entries = slice(h * HALF // LIST_ROWS, (h + 1) * HALF // LIST_ROWS)
+                    nc.vector.tensor_tensor(target[:, cols], ex_table[t][:].indirect(lst[:, entries]), other[:, cols], ALU.add)
+            den.append(total)
+
+        z_rows = keep.tile([P, PACK, S], BF16, name="z_rows")
+        for t in range(PACK):
+            root = keep.tile([P, S], F32, name=f"root{t}")
+            inv = keep.tile([P, S], F32, name=f"inv{t}")
+            parts = ((0, S),) if t < PACK - 1 else ((0, HALF), (HALF, HALF))
+            for c0, width in parts:
+                cols = slice(c0, c0 + width)
+                nc.scalar.activation(root[:, cols], den[t][:, cols], ACT.Abs_reciprocal_sqrt, scale=0.5)
+                nc.scalar.activation(inv[:, cols], root[:, cols], ACT.Square)
+                nc.vector.scalar_tensor_tensor(
+                    z_rows[:, t, cols], inv[:, cols], gn_sb[:, t : t + 1], ex_plain[t][:, cols], ALU.mult, ALU.mult
+                )
+
+        for c, (c0, width) in enumerate(CHUNKS):
+            z_grouped = keep.tile([P, width, PACK], BF16, name=f"z_grouped{c}", align_bytes=64)
+            nc.vector.tensor_copy(z_grouped[:], z_rows[:, :, c0 : c0 + width].rearrange("p t j -> p j t"))
+            z_codes = keep.tile([P, width], U32, name=f"z_codes{c}", align_bytes=64)
+            z_bytes = keep.tile([P, width], U8, name=f"z_bytes{c}", align_bytes=64)
+            nc.vector.quantize_mx(
+                out=z_codes[:].bitcast(FP8X4), scales=z_bytes[:], in_=z_grouped[:].rearrange("p j t -> p (j t)")
+            )
+            for u in range(2):
+                acc = psum.tile([P, 2, width], F32, name=f"acc{c}_{u}", tag=f"bank{(2 * c + u) % 4}")
+                for v in range(2):
+                    cols = slice((2 * u + v) * P, (2 * u + v + 1) * P)
+                    nc.tensor.matmul_mx(
+                        out=acc[:, v, :],
+                        lhsT=w_codes[:, cols].bitcast(FP8X4),
+                        lhsT_scale=w_bytes[:, cols],
+                        rhs=z_codes[:].bitcast(FP8X4),
+                        rhs_scale=z_bytes[:],
+                        start=True,
+                        stop=True,
+                    )
+                result = keep.tile([P, 2, width], F32, name=f"result{c}_{u}")
+                if c == len(CHUNKS) - 1 and u == 1:
+                    nc.vector.tensor_copy(result[:], acc[:])
+                else:
+                    nc.scalar.copy(result[:], acc[:])
+                nc.sync.dma_start(
+                    out[2 * u * P : (2 * u + 2) * P, c0 : c0 + width].rearrange("(v p) j -> p v j", v=2), result[:]
+                )

@@ -20,6 +20,8 @@ PACK = 4
 LIST_ROWS = 16
 HALF = S // 2
 CHUNKS = ((0, 256), (256, 128), (384, 128))
+VECTOR_TILES = 2
+UNITS = ((0, 0), (0, 1), (1, 0), (2, 0), (3, 0), (1, 1), (2, 1), (3, 1))
 W_PIECES = 2
 
 
@@ -28,6 +30,7 @@ def tile_picked_localsm_none_p_kernel(tc, x_words, x_scales, d_words, d_scales, 
     with ExitStack() as ctx:
         lists = ctx.enter_context(tc.tile_pool(name="lists", bufs=1))
         keep = ctx.enter_context(tc.tile_pool(name="keep", bufs=1))
+        ring = ctx.enter_context(tc.tile_pool(name="ring", bufs=2))
         psum = ctx.enter_context(tc.psum_pool(name="psum", bufs=1))
 
         kidx_sb = lists.tile([P, H // LIST_ROWS], U16, name="kidx_sb")
@@ -66,8 +69,8 @@ def tile_picked_localsm_none_p_kernel(tc, x_words, x_scales, d_words, d_scales, 
         nc.vector.tensor_copy(x_bytes_picked[:], x_byte_table[:].indirect(offs_sb[:]))
         planes = keep.tile([P, H + S], U8, name="planes", align_bytes=64)
         nc.vector.tensor_copy(
-            planes[:, :H].rearrange("p (t m) -> p m t", t=PACK),
-            d_bytes_picked[:].rearrange("p (m t) -> p m t", t=PACK),
+            planes[:, :H].rearrange("p (t m) -> p t m", t=PACK),
+            d_bytes_picked[:].rearrange("p (m t) -> p t m", t=PACK),
         )
         nc.vector.tensor_copy(planes[:, H:].bitcast(I32), x_bytes_picked[:].bitcast(I32))
         for r in range(1, 4):
@@ -114,36 +117,63 @@ def tile_picked_localsm_none_p_kernel(tc, x_words, x_scales, d_words, d_scales, 
                 stop=True,
             )
             table = keep.tile([P, S], F32, name=f"ex_table{t}")
-            plain = keep.tile([P, S], F32, name=f"ex_plain{t}")
+            second = keep.tile([P, S], F32, name=f"second{t}")
             nc.scalar.activation(table[:], scores[:], ACT.Exp, scale=0.03125)
-            nc.scalar.activation(plain[:], scores[:], ACT.Exp, scale=0.03125)
+            if t < VECTOR_TILES:
+                nc.scalar.activation(second[:], scores[:], ACT.Exp, scale=0.03125)
+            else:
+                nc.scalar.copy(second[:], scores[:])
             ex_table.append(table)
-            ex_plain.append(plain)
+            ex_plain.append(second)
 
-        den = []
-        for t in range(PACK):
-            pair = keep.tile([P, S], F32, name=f"pair{t}")
-            total = keep.tile([P, S], F32, name=f"den{t}")
-            for other, target, lst in ((ex_plain[t], pair, n1_sb), (pair, total, n2_sb)):
-                for h in range(2):
-                    cols = slice(h * HALF, (h + 1) * HALF)
-                    entries = slice(h * HALF // LIST_ROWS, (h + 1) * HALF // LIST_ROWS)
-                    nc.vector.tensor_tensor(target[:, cols], ex_table[t][:].indirect(lst[:, entries]), other[:, cols], ALU.add)
-            den.append(total)
+        def half(h):
+            return slice(h * HALF, (h + 1) * HALF)
+
+        def entries(h):
+            return slice(h * HALF // LIST_ROWS, (h + 1) * HALF // LIST_ROWS)
+
+        far = {}
+        for h in range(2):
+            for t in range(VECTOR_TILES, PACK):
+                fetched = keep.tile([P, HALF], F32, name=f"far{t}_{h}")
+                nc.scalar.activation(fetched[:], ex_plain[t][:].indirect(n2_sb[:, entries(h)]), ACT.Exp, scale=0.03125)
+                far[t, h] = fetched
+
+        den = [keep.tile([P, PACK, HALF], F32, name=f"den{h}") for h in range(2)]
+        pairs = {}
+
+        def first_sum(t, h):
+            pair = ring.tile([P, HALF], F32, name="pair")
+            other = ex_plain[t][:, half(h)] if t < VECTOR_TILES else far[t, h][:]
+            nc.vector.tensor_tensor(pair[:], ex_table[t][:].indirect(n1_sb[:, entries(h)]), other, ALU.add)
+            pairs[t, h] = pair
+
+        def second_sum(t, h):
+            other = ex_table[t][:].indirect(n2_sb[:, entries(h)]) if t < VECTOR_TILES else ex_table[t][:, half(h)]
+            nc.vector.tensor_tensor(den[h][:, t, :], other, pairs[t, h][:], ALU.add)
+
+        first_sum(*UNITS[0])
+        for unit, ahead in zip(UNITS, UNITS[1:]):
+            first_sum(*ahead)
+            second_sum(*unit)
+        second_sum(*UNITS[-1])
 
         z_rows = keep.tile([P, PACK, S], BF16, name="z_rows")
-        for t in range(PACK):
-            root = keep.tile([P, S], F32, name=f"root{t}")
-            inv = keep.tile([P, S], F32, name=f"inv{t}")
-            parts = ((0, S),) if t < PACK - 1 else ((0, HALF), (HALF, HALF))
-            for c0, width in parts:
-                cols = slice(c0, c0 + width)
-                nc.scalar.activation(root[:, cols], den[t][:, cols], ACT.Abs_reciprocal_sqrt, scale=0.5)
-                nc.scalar.activation(inv[:, cols], root[:, cols], ACT.Square)
-                nc.vector.scalar_tensor_tensor(
-                    z_rows[:, t, cols], inv[:, cols], gn_sb[:, t : t + 1], ex_plain[t][:, cols], ALU.mult, ALU.mult
-                )
 
+        def weigh(h):
+            root = keep.tile([P, PACK, HALF], F32, name=f"root{h}")
+            inv = keep.tile([P, PACK, HALF], F32, name=f"inv{h}")
+            for u in range(2):
+                two = slice(2 * u, 2 * u + 2)
+                nc.scalar.activation(root[:, two, :], den[h][:, two, :], ACT.Abs_reciprocal_sqrt, scale=0.5)
+                nc.scalar.activation(inv[:, two, :], root[:, two, :], ACT.Square)
+                for t in range(2 * u, 2 * u + 2):
+                    nc.vector.scalar_tensor_tensor(
+                        z_rows[:, t, half(h)], inv[:, t, :], gn_sb[:, t : t + 1], ex_table[t][:, half(h)], ALU.mult, ALU.mult
+                    )
+
+        weigh(0)
+        weigh(1)
         for c, (c0, width) in enumerate(CHUNKS):
             z_grouped = keep.tile([P, width, PACK], BF16, name=f"z_grouped{c}", align_bytes=64)
             nc.vector.tensor_copy(z_grouped[:], z_rows[:, :, c0 : c0 + width].rearrange("p t j -> p j t"))

@@ -18,15 +18,24 @@ ALU = mybir.AluOpType
 P = 128
 PACK = 4
 LIST_ROWS = 16
+BLOCK_ROWS = 8
+QUADRANT = 32
 HALF = S // 2
-CHUNKS = ((0, 256), (256, 128), (384, 128))
+EXP_SCALE = 0.5 * 0.0625
 VECTOR_TILES = 2
-UNITS = ((0, 0), (0, 1), (1, 0), (2, 0), (3, 0), (1, 1), (2, 1), (3, 1))
-W_PIECES = 2
+UNITS = ((0, 0), (0, 1), (1, 0), (1, 1), (2, 0), (3, 0), (2, 1), (3, 1))
+CHUNKS = ((0, 256), (256, 128), (384, 128))
 
 
 def tile_picked_localsm_none_p_kernel(tc, x_words, x_scales, d_words, d_scales, gn, w1, offs, kidx, n1, n2, out):
     nc = tc.nc
+
+    def half(h):
+        return slice(h * HALF, (h + 1) * HALF)
+
+    def entries(h):
+        return slice(h * HALF // LIST_ROWS, (h + 1) * HALF // LIST_ROWS)
+
     with ExitStack() as ctx:
         lists = ctx.enter_context(tc.tile_pool(name="lists", bufs=1))
         keep = ctx.enter_context(tc.tile_pool(name="keep", bufs=1))
@@ -38,52 +47,48 @@ def tile_picked_localsm_none_p_kernel(tc, x_words, x_scales, d_words, d_scales, 
         n1_sb = lists.tile([P, S // LIST_ROWS], U16, name="n1_sb")
         n2_sb = lists.tile([P, S // LIST_ROWS], U16, name="n2_sb")
         d_byte_table = keep.tile([P, G], U8, name="d_byte_table")
-        x_byte_table = keep.tile([P, T], U8, name="x_byte_table", tag="x_bytes_then_gn")
+        x_byte_table = keep.tile([P, T], U8, name="x_byte_table")
         d_word_table = keep.tile([P, G], U32, name="d_word_table")
         x_word_table = keep.tile([P, T], U32, name="x_word_table", tag="x_words_then_w", align_bytes=64)
+        gn_sb = keep.tile([P, PACK], F32, name="gn_sb")
 
+        nc.vector.memset(d_byte_table[:].bitcast(I32), 0)
+        nc.gpsimd.memset(x_byte_table[:].bitcast(I32), 0)
         nc.sync.dma_start(kidx_sb[:], kidx)
-        nc.sync.dma_start(
-            d_byte_table[:].bitcast(I32),
-            d_scales[0].bitcast(I32).unsqueeze(1).to_broadcast([16, 8, G // 4]),
-        )
+        nc.sync.dma_start(d_byte_table[0:P:BLOCK_ROWS, :].bitcast(I32), d_scales[0].bitcast(I32))
         nc.sync.dma_start(offs_sb[:], offs)
-        nc.sync.dma_start(
-            x_byte_table[:].bitcast(I32),
-            x_scales[0].bitcast(I32).unsqueeze(1).to_broadcast([16, 8, T // 4]),
-        )
+        nc.sync.dma_start(x_byte_table[0:P:BLOCK_ROWS, :].bitcast(I32), x_scales[0].bitcast(I32))
         nc.sync.dma_start(n1_sb[:], n1)
         nc.sync.dma_start(n2_sb[:], n2)
+        nc.sync.dma_start(gn_sb[:], gn.rearrange("(p t) o -> p (t o)", t=PACK))
         nc.sync.dma_start(d_word_table[:].bitcast(I32), d_words[0].rearrange("p n r -> p (n r)").bitcast(I32))
         nc.sync.dma_start(x_word_table[:].bitcast(I32), x_words[0].rearrange("p n r -> p (n r)").bitcast(I32))
-        w_width = N // W_PIECES
-        w_raw = []
-        for piece in range(W_PIECES):
-            raw = keep.tile([P, PACK, w_width], F32, name=f"w_raw{piece}")
-            nc.sync.dma_start(raw[:], w1[:, piece * w_width : (piece + 1) * w_width].rearrange("(p j) n -> p j n", j=PACK))
-            w_raw.append(raw)
+        w_first = keep.tile([P, PACK, N // 2], F32, name="w_first")
+        nc.sync.dma_start(w_first[:], w1[:, : N // 2].rearrange("(p j) n -> p j n", j=PACK))
 
         d_bytes_picked = keep.tile([P, H], U8, name="d_bytes_picked")
         nc.vector.tensor_copy(d_bytes_picked[:], d_byte_table[:].indirect(kidx_sb[:]))
-        x_bytes_picked = keep.tile([P, S], U8, name="x_bytes_picked")
+        x_bytes_picked = keep.tile([P, S], U8, name="x_bytes_picked", tag="x_bytes_then_w")
         nc.vector.tensor_copy(x_bytes_picked[:], x_byte_table[:].indirect(offs_sb[:]))
         planes = keep.tile([P, H + S], U8, name="planes", align_bytes=64)
         nc.vector.tensor_copy(
-            planes[:, :H].rearrange("p (t m) -> p t m", t=PACK),
-            d_bytes_picked[:].rearrange("p (m t) -> p t m", t=PACK),
+            planes[:, :H].rearrange("p (t c i) -> p c t i", t=PACK, i=16),
+            d_bytes_picked[:].rearrange("p (c i t) -> p c t i", t=PACK, i=16),
         )
         nc.vector.tensor_copy(planes[:, H:].bitcast(I32), x_bytes_picked[:].bitcast(I32))
-        for r in range(1, 4):
-            nc.scalar.dma_start(planes[r:P:32, :].bitcast(I32), planes[8 * r : P : 32, :].bitcast(I32))
-        gn_sb = keep.tile([P, PACK], F32, name="gn_sb", tag="x_bytes_then_gn")
-        nc.sync.dma_start(gn_sb[:], gn.rearrange("(p t) o -> p (t o)", t=PACK))
+        for r in range(1, QUADRANT // BLOCK_ROWS):
+            nc.scalar.dma_start(
+                planes[r:P:QUADRANT, :].bitcast(I32), planes[BLOCK_ROWS * r : P : QUADRANT, :].bitcast(I32)
+            )
+        w_second = keep.tile([P, PACK, N // 2], F32, name="w_second", tag="x_bytes_then_w")
+        nc.scalar.dma_start(w_second[:], w1[:, N // 2 :].rearrange("(p j) n -> p j n", j=PACK))
 
         d_codes_picked = keep.tile([P, H], U32, name="d_codes_picked")
         nc.vector.tensor_copy(d_codes_picked[:], d_word_table[:].indirect(kidx_sb[:]))
         d_codes = keep.tile([P, H], U32, name="d_codes", align_bytes=64)
         nc.vector.tensor_copy(
-            d_codes[:].rearrange("p (t m) -> p t m", t=PACK),
-            d_codes_picked[:].rearrange("p (m t) -> p t m", t=PACK),
+            d_codes[:].rearrange("p (t c i) -> p c t i", t=PACK, i=4),
+            d_codes_picked[:].rearrange("p (c i t) -> p c t i", t=PACK, i=4),
         )
         x_codes = keep.tile([P, S], U32, name="x_codes", align_bytes=64)
         nc.vector.tensor_copy(x_codes[:], x_word_table[:].indirect(offs_sb[:]))
@@ -91,11 +96,12 @@ def tile_picked_localsm_none_p_kernel(tc, x_words, x_scales, d_words, d_scales, 
         w_codes = keep.tile([P, N], U32, name="w_codes", align_bytes=64)
         w_bytes = keep.tile([P, N], U8, name="w_bytes", align_bytes=64)
         w_grouped = keep.tile([P, N, PACK], BF16, name="w_grouped", tag="x_words_then_w", align_bytes=64)
-        for piece in range(W_PIECES):
-            cols = slice(piece * w_width, (piece + 1) * w_width)
-            nc.vector.tensor_copy(w_grouped[:, cols, :], w_raw[piece][:].rearrange("p j n -> p n j"))
-        for piece in range(W_PIECES):
-            cols = slice(piece * w_width, (piece + 1) * w_width)
+        for piece, raw in enumerate((w_first, w_second)):
+            cols = slice(piece * N // 2, (piece + 1) * N // 2)
+            nc.vector.tensor_copy(
+                w_grouped[:, cols, :].rearrange("p (c i) j -> p c j i", i=4),
+                raw[:].rearrange("p j (c i) -> p c j i", i=4),
+            )
             nc.vector.quantize_mx(
                 out=w_codes[:, cols].bitcast(FP8X4),
                 scales=w_bytes[:, cols],
@@ -103,7 +109,7 @@ def tile_picked_localsm_none_p_kernel(tc, x_words, x_scales, d_words, d_scales, 
             )
 
         ex_table = []
-        ex_plain = []
+        second = []
         for t in range(PACK):
             keys = slice(t * P, (t + 1) * P)
             scores = psum.tile([P, S], F32, name=f"scores{t}")
@@ -117,40 +123,34 @@ def tile_picked_localsm_none_p_kernel(tc, x_words, x_scales, d_words, d_scales, 
                 stop=True,
             )
             table = keep.tile([P, S], F32, name=f"ex_table{t}")
-            second = keep.tile([P, S], F32, name=f"second{t}")
-            nc.scalar.activation(table[:], scores[:], ACT.Exp, scale=0.03125)
+            other = keep.tile([P, S], F32, name=f"second{t}")
+            nc.scalar.activation(table[:], scores[:], ACT.Exp, scale=EXP_SCALE)
             if t < VECTOR_TILES:
-                nc.scalar.activation(second[:], scores[:], ACT.Exp, scale=0.03125)
+                nc.scalar.activation(other[:], scores[:], ACT.Exp, scale=EXP_SCALE)
             else:
-                nc.scalar.copy(second[:], scores[:])
+                nc.scalar.copy(other[:], scores[:])
             ex_table.append(table)
-            ex_plain.append(second)
-
-        def half(h):
-            return slice(h * HALF, (h + 1) * HALF)
-
-        def entries(h):
-            return slice(h * HALF // LIST_ROWS, (h + 1) * HALF // LIST_ROWS)
+            second.append(other)
 
         far = {}
         for h in range(2):
             for t in range(VECTOR_TILES, PACK):
                 fetched = keep.tile([P, HALF], F32, name=f"far{t}_{h}")
-                nc.scalar.activation(fetched[:], ex_plain[t][:].indirect(n2_sb[:, entries(h)]), ACT.Exp, scale=0.03125)
+                nc.scalar.activation(fetched[:], second[t][:].indirect(n2_sb[:, entries(h)]), ACT.Exp, scale=EXP_SCALE)
                 far[t, h] = fetched
 
-        den = [keep.tile([P, PACK, HALF], F32, name=f"den{h}") for h in range(2)]
+        den = keep.tile([P, PACK, S], F32, name="den")
         pairs = {}
 
         def first_sum(t, h):
             pair = ring.tile([P, HALF], F32, name="pair")
-            other = ex_plain[t][:, half(h)] if t < VECTOR_TILES else far[t, h][:]
-            nc.vector.tensor_tensor(pair[:], ex_table[t][:].indirect(n1_sb[:, entries(h)]), other, ALU.add)
+            plain = second[t][:, half(h)] if t < VECTOR_TILES else far[t, h][:]
+            nc.vector.tensor_tensor(pair[:], ex_table[t][:].indirect(n1_sb[:, entries(h)]), plain, ALU.add)
             pairs[t, h] = pair
 
         def second_sum(t, h):
-            other = ex_table[t][:].indirect(n2_sb[:, entries(h)]) if t < VECTOR_TILES else ex_table[t][:, half(h)]
-            nc.vector.tensor_tensor(den[h][:, t, :], other, pairs[t, h][:], ALU.add)
+            third = ex_table[t][:].indirect(n2_sb[:, entries(h)]) if t < VECTOR_TILES else ex_table[t][:, half(h)]
+            nc.vector.tensor_tensor(den[:, t, half(h)], third, pairs[t, h][:], ALU.add)
 
         first_sum(*UNITS[0])
         for unit, ahead in zip(UNITS, UNITS[1:]):
@@ -158,25 +158,26 @@ def tile_picked_localsm_none_p_kernel(tc, x_words, x_scales, d_words, d_scales, 
             second_sum(*unit)
         second_sum(*UNITS[-1])
 
+        root = keep.tile([P, PACK, S], F32, name="root")
+        inv = keep.tile([P, PACK, S], F32, name="inv")
         z_rows = keep.tile([P, PACK, S], BF16, name="z_rows")
-
-        def weigh(h):
-            root = keep.tile([P, PACK, HALF], F32, name=f"root{h}")
-            inv = keep.tile([P, PACK, HALF], F32, name=f"inv{h}")
-            for u in range(2):
-                two = slice(2 * u, 2 * u + 2)
-                nc.scalar.activation(root[:, two, :], den[h][:, two, :], ACT.Abs_reciprocal_sqrt, scale=0.5)
-                nc.scalar.activation(inv[:, two, :], root[:, two, :], ACT.Square)
-                for t in range(2 * u, 2 * u + 2):
+        for h in range(2):
+            for t0 in range(0, PACK, 2):
+                two = slice(t0, t0 + 2)
+                nc.scalar.activation(root[:, two, half(h)], den[:, two, half(h)], ACT.Abs_reciprocal_sqrt, scale=0.5)
+                nc.scalar.activation(inv[:, two, half(h)], root[:, two, half(h)], ACT.Square)
+                for t in range(t0, t0 + 2):
                     nc.vector.scalar_tensor_tensor(
-                        z_rows[:, t, half(h)], inv[:, t, :], gn_sb[:, t : t + 1], ex_table[t][:, half(h)], ALU.mult, ALU.mult
+                        z_rows[:, t, half(h)], inv[:, t, half(h)], gn_sb[:, t : t + 1], ex_table[t][:, half(h)], ALU.mult, ALU.mult
                     )
 
-        weigh(0)
-        weigh(1)
         for c, (c0, width) in enumerate(CHUNKS):
+            last = c == len(CHUNKS) - 1
             z_grouped = keep.tile([P, width, PACK], BF16, name=f"z_grouped{c}", align_bytes=64)
-            nc.vector.tensor_copy(z_grouped[:], z_rows[:, :, c0 : c0 + width].rearrange("p t j -> p j t"))
+            nc.vector.tensor_copy(
+                z_grouped[:].rearrange("p (c i) t -> p c t i", i=4),
+                z_rows[:, :, c0 : c0 + width].rearrange("p t (c i) -> p c t i", i=4),
+            )
             z_codes = keep.tile([P, width], U32, name=f"z_codes{c}", align_bytes=64)
             z_bytes = keep.tile([P, width], U8, name=f"z_bytes{c}", align_bytes=64)
             nc.vector.quantize_mx(
@@ -196,10 +197,11 @@ def tile_picked_localsm_none_p_kernel(tc, x_words, x_scales, d_words, d_scales, 
                         stop=True,
                     )
                 result = keep.tile([P, 2, width], F32, name=f"result{c}_{u}")
-                if c == len(CHUNKS) - 1 and u == 1:
+                if last and u == 1:
                     nc.vector.tensor_copy(result[:], acc[:])
                 else:
                     nc.scalar.copy(result[:], acc[:])
-                nc.sync.dma_start(
+                queue = nc.scalar if last and u == 0 else nc.sync
+                queue.dma_start(
                     out[2 * u * P : (2 * u + 2) * P, c0 : c0 + width].rearrange("(v p) j -> p v j", v=2), result[:]
                 )

from contextlib import ExitStack

import concourse.mybir as mybir

K, T, S, N, G, H = 512, 2048, 512, 512, 2048, 512
FLOPS = 2 * K * H * S + 2 * H * N * S

F32 = mybir.dt.float32
BF16 = mybir.dt.bfloat16
I32 = mybir.dt.int32
U32 = mybir.dt.uint32
U16 = mybir.dt.uint16
U8 = mybir.dt.uint8
FP8X4 = mybir.dt.float8_e4m3fn_x4
ACT = mybir.ActivationFunctionType
ALU = mybir.AluOpType

P = 128
PACK = 4
LIST_ROWS = 16
BLOCK_ROWS = 8
QUADRANT = 32
HALF = S // 2
EXP_SCALE = 0.5 * 0.0625
VECTOR_TILES = 2
UNITS = ((0, 0), (0, 1), (1, 0), (1, 1), (2, 0), (3, 0), (2, 1), (3, 1))
CHUNKS = ((0, 256), (256, 128), (384, 128))


def tile_picked_localsm_none_p_kernel(tc, x_words, x_scales, d_words, d_scales, gn, w1, offs, kidx, n1, n2, out):
    nc = tc.nc

    def half(h):
        return slice(h * HALF, (h + 1) * HALF)

    def entries(h):
        return slice(h * HALF // LIST_ROWS, (h + 1) * HALF // LIST_ROWS)

    with ExitStack() as ctx:
        lists = ctx.enter_context(tc.tile_pool(name="lists", bufs=1))
        keep = ctx.enter_context(tc.tile_pool(name="keep", bufs=1))
        ring = ctx.enter_context(tc.tile_pool(name="ring", bufs=2))
        psum = ctx.enter_context(tc.psum_pool(name="psum", bufs=1))

        kidx_sb = lists.tile([P, H // LIST_ROWS], U16, name="kidx_sb")
        offs_sb = lists.tile([P, S // LIST_ROWS], U16, name="offs_sb")
        n1_sb = lists.tile([P, S // LIST_ROWS], U16, name="n1_sb")
        n2_sb = lists.tile([P, S // LIST_ROWS], U16, name="n2_sb")
        d_byte_table = keep.tile([P, G], U8, name="d_byte_table")
        x_byte_table = keep.tile([P, T], U8, name="x_byte_table")
        d_word_table = keep.tile([P, G], U32, name="d_word_table")
        x_word_table = keep.tile([P, T], U32, name="x_word_table", tag="x_words_then_w", align_bytes=64)
        gn_sb = keep.tile([P, PACK], F32, name="gn_sb")

        nc.vector.memset(d_byte_table[:].bitcast(I32), 0)
        nc.gpsimd.memset(x_byte_table[:].bitcast(I32), 0)
        nc.sync.dma_start(kidx_sb[:], kidx)
        nc.sync.dma_start(d_byte_table[0:P:BLOCK_ROWS, :].bitcast(I32), d_scales[0].bitcast(I32))
        nc.sync.dma_start(offs_sb[:], offs)
        nc.sync.dma_start(x_byte_table[0:P:BLOCK_ROWS, :].bitcast(I32), x_scales[0].bitcast(I32))
        nc.sync.dma_start(n1_sb[:], n1)
        nc.sync.dma_start(n2_sb[:], n2)
        nc.sync.dma_start(gn_sb[:], gn.rearrange("(p t) o -> p (t o)", t=PACK))
        nc.sync.dma_start(d_word_table[:].bitcast(I32), d_words[0].rearrange("p n r -> p (n r)").bitcast(I32))
        nc.sync.dma_start(x_word_table[:].bitcast(I32), x_words[0].rearrange("p n r -> p (n r)").bitcast(I32))
        w_first = keep.tile([P, PACK, N // 2], F32, name="w_first")
        nc.sync.dma_start(w_first[:], w1[:, : N // 2].rearrange("(p j) n -> p j n", j=PACK))

        d_bytes_picked = keep.tile([P, H], U8, name="d_bytes_picked")
        nc.vector.tensor_copy(d_bytes_picked[:], d_byte_table[:].indirect(kidx_sb[:]))
        x_bytes_picked = keep.tile([P, S], U8, name="x_bytes_picked", tag="x_bytes_then_w")
        nc.vector.tensor_copy(x_bytes_picked[:], x_byte_table[:].indirect(offs_sb[:]))
        planes = keep.tile([P, H + S], U8, name="planes", align_bytes=64)
        nc.vector.tensor_copy(
            planes[:, :H].rearrange("p (t c i) -> p c t i", t=PACK, i=16),
            d_bytes_picked[:].rearrange("p (c i t) -> p c t i", t=PACK, i=16),
        )
        nc.vector.tensor_copy(planes[:, H:].bitcast(I32), x_bytes_picked[:].bitcast(I32))
        for r in range(1, QUADRANT // BLOCK_ROWS):
            nc.scalar.dma_start(
                planes[r:P:QUADRANT, :].bitcast(I32), planes[BLOCK_ROWS * r : P : QUADRANT, :].bitcast(I32)
            )
        w_second = keep.tile([P, PACK, N // 2], F32, name="w_second", tag="x_bytes_then_w")
        nc.scalar.dma_start(w_second[:], w1[:, N // 2 :].rearrange("(p j) n -> p j n", j=PACK))

        d_codes_picked = keep.tile([P, H], U32, name="d_codes_picked")
        nc.vector.tensor_copy(d_codes_picked[:], d_word_table[:].indirect(kidx_sb[:]))
        d_codes = keep.tile([P, H], U32, name="d_codes", align_bytes=64)
        nc.vector.tensor_copy(
            d_codes[:].rearrange("p (t c i) -> p c t i", t=PACK, i=4),
            d_codes_picked[:].rearrange("p (c i t) -> p c t i", t=PACK, i=4),
        )
        x_codes = keep.tile([P, S], U32, name="x_codes", align_bytes=64)
        nc.vector.tensor_copy(x_codes[:], x_word_table[:].indirect(offs_sb[:]))

        w_codes = keep.tile([P, N], U32, name="w_codes", align_bytes=64)
        w_bytes = keep.tile([P, N], U8, name="w_bytes", align_bytes=64)
        w_grouped = keep.tile([P, N, PACK], BF16, name="w_grouped", tag="x_words_then_w", align_bytes=64)
        for piece, raw in enumerate((w_first, w_second)):
            cols = slice(piece * N // 2, (piece + 1) * N // 2)
            nc.vector.tensor_copy(
                w_grouped[:, cols, :].rearrange("p (c i) j -> p c j i", i=4),
                raw[:].rearrange("p j (c i) -> p c j i", i=4),
            )
            nc.vector.quantize_mx(
                out=w_codes[:, cols].bitcast(FP8X4),
                scales=w_bytes[:, cols],
                in_=w_grouped[:, cols, :].rearrange("p n j -> p (n j)"),
            )

        ex_table = []
        second = []
        for t in range(PACK):
            keys = slice(t * P, (t + 1) * P)
            scores = psum.tile([P, S], F32, name=f"scores{t}")
            nc.tensor.matmul_mx(
                out=scores[:],
                lhsT=d_codes[:, keys].bitcast(FP8X4),
                lhsT_scale=planes[:, keys],
                rhs=x_codes[:].bitcast(FP8X4),
                rhs_scale=planes[:, H:],
                start=True,
                stop=True,
            )
            table = keep.tile([P, S], F32, name=f"ex_table{t}")
            other = keep.tile([P, S], F32, name=f"second{t}")
            nc.scalar.activation(table[:], scores[:], ACT.Exp, scale=EXP_SCALE)
            if t < VECTOR_TILES:
                nc.scalar.activation(other[:], scores[:], ACT.Exp, scale=EXP_SCALE)
            else:
                nc.scalar.copy(other[:], scores[:])
            ex_table.append(table)
            second.append(other)

        far = {}
        for h in range(2):
            for t in range(VECTOR_TILES, PACK):
                fetched = keep.tile([P, HALF], F32, name=f"far{t}_{h}")
                nc.scalar.activation(fetched[:], second[t][:].indirect(n2_sb[:, entries(h)]), ACT.Exp, scale=EXP_SCALE)
                far[t, h] = fetched

        den = keep.tile([P, PACK, S], F32, name="den")
        pairs = {}

        def first_sum(t, h):
            pair = ring.tile([P, HALF], F32, name="pair")
            plain = second[t][:, half(h)] if t < VECTOR_TILES else far[t, h][:]
            nc.vector.tensor_tensor(pair[:], ex_table[t][:].indirect(n1_sb[:, entries(h)]), plain, ALU.add)
            pairs[t, h] = pair

        def second_sum(t, h):
            third = ex_table[t][:].indirect(n2_sb[:, entries(h)]) if t < VECTOR_TILES else ex_table[t][:, half(h)]
            nc.vector.tensor_tensor(den[:, t, half(h)], third, pairs[t, h][:], ALU.add)

        first_sum(*UNITS[0])
        for unit, ahead in zip(UNITS, UNITS[1:]):
            first_sum(*ahead)
            second_sum(*unit)
        second_sum(*UNITS[-1])

        root = keep.tile([P, PACK, S], F32, name="root")
        inv = keep.tile([P, PACK, S], F32, name="inv")
        z_rows = keep.tile([P, PACK, S], BF16, name="z_rows")
        for h in range(2):
            for t0 in range(0, PACK, 2):
                two = slice(t0, t0 + 2)
                nc.scalar.activation(root[:, two, half(h)], den[:, two, half(h)], ACT.Abs_reciprocal_sqrt, scale=0.5)
                nc.scalar.activation(inv[:, two, half(h)], root[:, two, half(h)], ACT.Square)
                for t in range(t0, t0 + 2):
                    nc.vector.scalar_tensor_tensor(
                        z_rows[:, t, half(h)], inv[:, t, half(h)], gn_sb[:, t : t + 1], ex_table[t][:, half(h)], ALU.mult, ALU.mult
                    )

        for c, (c0, width) in enumerate(CHUNKS):
            last = c == len(CHUNKS) - 1
            z_grouped = keep.tile([P, width, PACK], BF16, name=f"z_grouped{c}", align_bytes=64)
            nc.vector.tensor_copy(
                z_grouped[:].rearrange("p (c i) t -> p c t i", i=4),
                z_rows[:, :, c0 : c0 + width].rearrange("p t (c i) -> p c t i", i=4),
            )
            z_codes = keep.tile([P, width], U32, name=f"z_codes{c}", align_bytes=64)
            z_bytes = keep.tile([P, width], U8, name=f"z_bytes{c}", align_bytes=64)
            nc.vector.quantize_mx(
                out=z_codes[:].bitcast(FP8X4), scales=z_bytes[:], in_=z_grouped[:].rearrange("p j t -> p (j t)")
            )
            for u in range(2):
                acc = psum.tile([P, 2, width], F32, name=f"acc{c}_{u}", tag=f"bank{(2 * c + u) % 4}")
                for v in range(2):
                    cols = slice((2 * u + v) * P, (2 * u + v + 1) * P)
                    nc.tensor.matmul_mx(
                        out=acc[:, v, :],
                        lhsT=w_codes[:, cols].bitcast(FP8X4),
                        lhsT_scale=w_bytes[:, cols],
                        rhs=z_codes[:].bitcast(FP8X4),
                        rhs_scale=z_bytes[:],
                        start=True,
                        stop=True,
                    )
                result = keep.tile([P, 2, width], F32, name=f"result{c}_{u}")
                if last and u == 1:
                    nc.vector.tensor_copy(result[:], acc[:])
                else:
                    nc.scalar.copy(result[:], acc[:])
                queue = nc.scalar if last and u == 0 else nc.sync
                queue.dma_start(
                    out[2 * u * P : (2 * u + 2) * P, c0 : c0 + width].rearrange("(v p) j -> p v j", v=2), result[:]
                )
